import numpy as np, ml_dtypes
CORES = [24,32,56,88,96,104,30,38,62,94,102,110]
N = 12
KT, HT, TK = 1, 4, 128
def setup_inputs(rng):
    w = (rng.standard_normal((128, KT * HT * 128), dtype=np.float32) / 8).astype(ml_dtypes.bfloat16)
    return {"x": rng.standard_normal((N, 128, KT * TK), dtype=np.float32).astype(ml_dtypes.bfloat16), "w": np.broadcast_to(w, (N,) + w.shape).copy()}
def setup_inputs_big(rng):
    d = setup_inputs(rng)
    for k in ("x", "w"): d[k] = (d[k].astype(np.float32) * 1024.0).astype(d[k].dtype)
    return d
def setup_inputs_small(rng):
    d = setup_inputs(rng)
    for k in ("x", "w"): d[k] = (d[k].astype(np.float32) * (1 / 1024.0)).astype(d[k].dtype)
    return d
def setup_inputs_apart(rng):
    d = setup_inputs(rng)
    f = (10.0 ** rng.permutation(np.linspace(-1.5, 1.5, N))).astype(np.float32).reshape(N, 1, 1)
    for k in ("x",): d[k] = (d[k].astype(np.float32) * f).astype(d[k].dtype)
    return d
def tie_inputs(x):
    x = dict(x)
    x["w"] = np.broadcast_to(x["w"][0], x["w"].shape).copy()
    return x
def reference(x, w):
    X, W = x.astype(np.float64), w.astype(np.float64)
    def hidden(r):
        return np.stack([np.maximum(sum(W[r][:, 128 * (HT * t + u):128 * (HT * t + u) + 128].T @ X[r][:, TK * t:TK * t + TK] for t in range(KT)), 0.0) for u in range(HT)])
    h = [hidden(r) for r in range(N)]
    y = np.stack([sum(h[(r - 1) % N][u].T @ h[r][u] for u in range(HT)) for r in range(N)])
    return {"y": y.astype(ml_dtypes.bfloat16 if x.dtype != np.float64 else np.float64)}

from concourse.mybir import AluOpType

HT = 4
TK = 128
SIM_CORES = 112

SCRATCH = {
    "xd": ("dram", [128, TK], "bfloat16"),
    "rx": ("dram", [128, TK], "bfloat16"),
    "xs": ("sbuf", [128, TK], "bfloat16"),
    "ws": ("sbuf", [128, HT * 128], "bfloat16"),
    "xp": ("sbuf", [128, TK], "bfloat16"),
    "zz": ("sbuf", [128, HT * TK], "float32"),
    "hr": ("sbuf", [128, HT * TK], "bfloat16"),
    "hp": ("sbuf", [128, HT * TK], "bfloat16"),
    "ys": ("sbuf", [128, TK], "bfloat16"),
    "pr": ("psum", [128, 512], "float32"),
    "pp0": ("psum", [128, 512], "float32"),
    "pp1": ("psum", [128, 512], "float32"),
    "pp2": ("psum", [128, 512], "float32"),
    "pp3": ("psum", [128, 512], "float32"),
    "py": ("psum", [128, 512], "float32"),
}
SEMAPHORES = ["xdl", "xsl", "wl", "zs", "mr", "rr", "mp0", "mp1", "mp2", "mp3", "rp0", "rp1", "rp2", "rp3",
              "my", "yc", "st", "arr", "rel", "sent"]

HOP_ENGINES = 4


def _pick(mask, k):
    bits = [b for b in range(mask.bit_length()) if (mask >> b) & 1]
    k = min(k, len(bits))
    step = len(bits) // k
    out = 0
    for b in bits[::step][:k]:
        out |= 1 << b
    return out


def _count(mask):
    return bin(mask).count("1")


def _ways(T, topo):
    cores = list(T.cores)
    n = len(cores)
    ways = []
    for i, s in enumerate(cores):
        d = cores[(i + 1) % n]
        relay = None
        if not topo.may_write(s, d):
            near = [c for c in range(SIM_CORES)
                    if c != s and c != d and topo.chip(c) == topo.chip(s) and topo.may_write(c, d)]
            ranks = [c for c in near if c in cores]
            relay = (ranks or near)[0]
        ways.append((s, relay, d))
    return ways


def _send(g, T, topo, src, dst, out_ap, in_ap, sem, engines):
    rid, pid, _ = topo.addr(dst)
    m = _pick(topo.mask(src, dst), engines)
    g.remote_dma(out_ap=out_ap, in_ap=in_ap, remote_sem=sem, local_sem=T.sem.sent,
                 pid=pid, routing_id=rid, dma_engine_mask=m)
    return _count(m)


def rank_program(g, core, T, topo):
    ways = _ways(T, topo)
    rank = T.rank_of(core)
    passes = [w for w in ways if w[1] == core]
    sent = 0

    if rank is not None:
        g.sync.dma_start(T.xd[:], T.x[:]).then_inc(T.sem.xdl, 16)
        g.scalar.dma_start(T.xs[:], T.x[:]).then_inc(T.sem.xsl, 16)
        g.sync.dma_start(T.ws[:], T.w[:]).then_inc(T.sem.wl, 16)

        s, relay, d = ways[rank]
        g.wait_ge(T.sem.xdl, 16)
        if relay is None:
            sent += _send(g, T, topo, core, d, T.xp[:], T.xd[:], T.sem.arr, 16)
        else:
            sent += _send(g, T, topo, core, relay, T.rx[:], T.xd[:], T.sem.rel, HOP_ENGINES)

    for (s, relay, d) in passes:
        g.wait_ge(T.sem.rel, _count(_pick(topo.mask(s, core), HOP_ENGINES)))
        sent += _send(g, T, topo, core, d, T.xp[:], T.rx[:], T.sem.arr, 16)
    if sent:
        g.wait_ge(T.sem.sent, sent)
    if rank is None:
        return

    ps, prelay, _ = ways[(rank - 1) % len(ways)]
    last = ps if prelay is None else prelay
    n_arr = _count(_pick(topo.mask(last, core), 16))

    te, ve = g.tensor, g.vector
    pp = [T.pp0, T.pp1, T.pp2, T.pp3]
    mp = [T.sem.mp0, T.sem.mp1, T.sem.mp2, T.sem.mp3]
    rp = [T.sem.rp0, T.sem.rp1, T.sem.rp2, T.sem.rp3]

    def tile(t, u):
        return t[:, u * 128:(u + 1) * 128]

    te.wait_ge(T.sem.xsl, 16)
    te.wait_ge(T.sem.wl, 16)
    for u in range(HT):
        te.matmul(out=tile(T.pr, u), lhsT=tile(T.ws, u), rhs=T.xs[:], start=True, stop=True).then_inc(T.sem.mr, 1)
    te.wait_ge(T.sem.arr, n_arr)
    for u in range(HT):
        te.matmul(out=pp[u][:, 0:TK], lhsT=tile(T.ws, u), rhs=T.xp[:], start=True, stop=True).then_inc(mp[u], 1)
    te.wait_ge(T.sem.rr, 1)
    for u in range(HT):
        te.wait_ge(rp[u], 1)
        mm = te.matmul(out=T.py[:, 0:TK], lhsT=tile(T.hp, u), rhs=tile(T.hr, u), start=(u == 0), stop=(u == HT - 1))
        if u == HT - 1:
            mm.then_inc(T.sem.my, 1)

    ve.memset(T.zz[:], 0.0).then_inc(T.sem.zs, 1)
    ve.wait_ge(T.sem.zs, 1)
    ve.wait_ge(T.sem.mr, HT)
    ve.tensor_tensor(out=T.hr[:], in0=T.pr[:], in1=T.zz[:], op=AluOpType.max).then_inc(T.sem.rr, 1)
    for u in range(HT):
        ve.wait_ge(mp[u], 1)
        ve.tensor_tensor(out=tile(T.hp, u), in0=pp[u][:, 0:TK], in1=T.zz[:, 0:TK], op=AluOpType.max).then_inc(rp[u], 1)
    ve.wait_ge(T.sem.my, 1)
    ve.tensor_copy(out=T.ys[:], in_=T.py[:, 0:TK]).then_inc(T.sem.yc, 1)

    g.scalar.wait_ge(T.sem.yc, 1)
    g.scalar.dma_start(T.y[:], T.ys[:]).then_inc(T.sem.st, 16)
    g.scalar.wait_ge(T.sem.st, 16)
